import numpy as np
import ml_dtypes


def mxq(x, axis, fmt="e4m3"):
    dtype, down = {"e4m3": (ml_dtypes.float8_e4m3fn, 7), "e5m2": (ml_dtypes.float8_e5m2, 14)}[fmt]
    v = np.moveaxis(np.asarray(x, np.float32).astype(ml_dtypes.bfloat16).astype(np.float64), axis, -1)
    blocks = v.reshape(v.shape[:-1] + (-1, 32))
    amax = np.abs(blocks).max(-1, keepdims=True)
    byte = np.maximum(np.where(amax > 0, np.frexp(amax)[1] - 1 + 127, 0) - down, 1)
    scale = np.exp2(byte - 127.0)
    codes = (blocks / scale).astype(np.float32).astype(dtype).astype(np.float64)
    return np.moveaxis((codes * scale).reshape(v.shape), -1, axis)


WIDE = False


def mx_kscale(k):
    if not WIDE:
        return np.ones(k)
    levels = np.array([10, -10, 5, -5, 0])
    if k % 512:
        return np.exp2(np.random.permutation(np.resize(levels, k // 32))).repeat(32)
    a = np.empty((k // 512, 16))
    for p in range(k // 512):
        a[p, :8] = np.random.permutation(np.resize(levels, 8))
        for g in range(8):
            far = levels[np.abs(levels - a[p, g]) >= 10]
            a[p, g + 8] = far[np.random.randint(len(far))]
    return np.exp2(a.ravel()).repeat(32)


def f64(x):
    return np.asarray(x).astype(np.float64)


def striped(idx):
    return np.tile(idx.reshape(-1, 16).T, (8, 1)).astype(np.uint16)


def unstriped(offs):
    return offs[:16].T.reshape(-1).astype(np.int64)


def silu(v):
    return v / (1.0 + np.exp(-np.maximum(v, -700.0)))


K, T, D, S, V, H, N = 512, 2048, 4, 2048, 512, 512, 256


def setup_inputs():
    n = np.random.standard_normal
    s = mx_kscale(K)[:, None]
    u = mx_kscale(H)
    return {
        "xT": (n((K, T)) * s).astype(np.float32),
        "w1": (n((K, H)) / np.sqrt(K) / s * u).astype(np.float32),
        "w2": (n((H, N)) / np.sqrt(H) / u[:, None]).astype(np.float32),
        "offs": striped(np.concatenate([np.random.permutation(T)[:V] for _ in range(D)])),
    }


def reference(xT, w1, w2, offs):
    idx = unstriped(offs)
    x = np.empty((K, V))
    for l in range(D):
        r = l // 4 * (4 * K // D) + l % 4 + 4 * np.arange(K // D)
        x[r] = f64(xT)[r][:, idx[l * V:(l + 1) * V]]
    xq = mxq(x, 0, "e4m3")
    h = silu(mxq(f64(w1), 0, "e4m3").T @ xq)
    return mxq(f64(w2), 0, "e4m3").T @ mxq(h, 0, "e4m3")

@@ -1,0 +1,179 @@
+from contextlib import ExitStack
+
+import concourse.mybir as mybir
+
+K, T, D, V, H, N = 512, 2048, 4, 512, 512, 256
+FLOPS = 2 * K * H * V + 2 * H * N * V
+
+F32 = mybir.dt.float32
+BF16 = mybir.dt.bfloat16
+U32 = mybir.dt.uint32
+U16 = mybir.dt.uint16
+U8 = mybir.dt.uint8
+FP8X4 = mybir.dt.float8_e4m3fn_x4
+SILU = mybir.ActivationFunctionType.Silu
+
+P = 128
+HALF = V // 2
+
+
+def tile_picked_grid_mlp_silu_sub_l_kernel(tc, xT, w1, w2, offs, out):
+    nc = tc.nc
+    with ExitStack() as ctx:
+        keep = ctx.enter_context(tc.tile_pool(name="keep", bufs=1))
+        pre_pool = ctx.enter_context(tc.psum_pool(name="pre_pool", bufs=3))
+        acc_pool = ctx.enter_context(tc.psum_pool(name="acc_pool", bufs=3))
+        end_pool = ctx.enter_context(tc.psum_pool(name="end_pool", bufs=1))
+
+        offsets = keep.tile([P, D * V // 16], U16, name="offsets")
+        w1_raw = keep.tile([P, 4, H], F32, name="w1_raw")
+        w2_raw = keep.tile([P, 4, N], F32, name="w2_raw")
+        tables = [keep.tile([P, T], F32, name=f"table{l}") for l in range(D)]
+        w1_grp = keep.tile([P, 4 * H], BF16, name="w1_grp", align_bytes=64)
+        w2_grp = keep.tile([P, 4 * N], BF16, name="w2_grp", align_bytes=64)
+        x_grp = keep.tile([P, V, 4], BF16, name="x_grp", align_bytes=64)
+        w1_codes = keep.tile([P, H], U32, name="w1_codes", align_bytes=64)
+        w1_scales = keep.tile([P, H], U8, name="w1_scales", align_bytes=64)
+        w2_codes = keep.tile([P, N], U32, name="w2_codes", align_bytes=64)
+        w2_scales = keep.tile([P, N], U8, name="w2_scales", align_bytes=64)
+        x_codes = keep.tile([P, V], U32, name="x_codes", align_bytes=64)
+        x_scales = keep.tile([P, V], U8, name="x_scales", align_bytes=64)
+        dummy = keep.tile([P, 1], F32, name="dummy")
+        dummy_out = keep.tile([P, 1], F32, name="dummy_out")
+
+        nc.vector.memset(dummy[:], 0.0)
+        nc.scalar.activation(dummy_out[:], dummy[:], SILU)
+
+        x_levels = xT.rearrange("(f l) t -> l f t", l=D)
+        nc.sync.dma_start(offsets[:], offs)
+        nc.sync.dma_start(out=w1_raw[:], in_=w1.rearrange("(p j) i -> p j i", j=4))
+        for l in range(D):
+            nc.sync.dma_start(out=tables[l][:], in_=x_levels[l, :, :])
+        nc.sync.dma_start(out=w2_raw[:], in_=w2.rearrange("(p j) m -> p j m", j=4))
+
+        nc.scalar.copy(
+            out=w1_grp[:].rearrange("p (t m j) -> p m j t", t=4, j=4),
+            in_=w1_raw[:].rearrange("p j (m t) -> p m j t", t=4),
+        )
+
+        def gather(l, v0, n):
+            c0 = (l * V + v0) // 16
+            nc.vector.tensor_copy(
+                x_grp[:, v0 : v0 + n, l],
+                tables[l][:].indirect(offsets[:, c0 : c0 + n // 16]),
+            )
+
+        def quantize(codes, scales, grouped, a, b):
+            nc.vector.quantize_mx(
+                out=codes[:, a:b].bitcast(FP8X4), scales=scales[:, a:b], in_=grouped[:, 4 * a : 4 * b]
+            )
+
+        x_flat = x_grp[:].rearrange("p v j -> p (v j)")
+        out_view = out.rearrange("(b p) v -> p b v", p=P)
+        bounds = [(0, 128), (128, 256), (256, 384), (384, 448), (448, 512)]
+        last = len(bounds) - 1
+        h_tiles = {}
+        accs = {}
+
+        def first_product(s):
+            a, b = bounds[s]
+            n = b - a
+            pre = pre_pool.tile([P, 4, n], F32, name="pre")
+            for t in range(4):
+                cols = slice(t * P, (t + 1) * P)
+                nc.tensor.matmul_mx(
+                    out=pre[:, t, :],
+                    lhsT=w1_codes[:, cols].bitcast(FP8X4),
+                    lhsT_scale=w1_scales[:, cols],
+                    rhs=x_codes[:, a:b].bitcast(FP8X4),
+                    rhs_scale=x_scales[:, a:b],
+                    start=True,
+                    stop=True,
+                )
+            h_grp = keep.tile([P, 4 * n], BF16, name=f"h_grp{s}", align_bytes=64)
+            nc.scalar.activation(
+                h_grp[:].rearrange("p (v t) -> p v t", t=4), pre[:].rearrange("p t v -> p v t"), SILU
+            )
+            h_tiles[s] = [h_grp]
+
+        def quantize_h(s):
+            n = bounds[s][1] - bounds[s][0]
+            h_codes = keep.tile([P, n], U32, name=f"h_codes{s}", align_bytes=64)
+            h_scales = keep.tile([P, n], U8, name=f"h_scales{s}", align_bytes=64)
+            quantize(h_codes, h_scales, h_tiles[s][0], 0, n)
+            h_tiles[s] += [h_codes, h_scales]
+
+        def second_product(s):
+            n = bounds[s][1] - bounds[s][0]
+            if s < last:
+                acc = acc_pool.tile([P, 2, n], F32, name="acc")
+                sides = [acc[:, 0, :], acc[:, 1, :]]
+            else:
+                end0 = end_pool.tile([P, n], F32, name="end0")
+                end1 = end_pool.tile([P, n], F32, name="end1")
+                acc = (end0, end1)
+                sides = [end0[:], end1[:]]
+            for b in range(2):
+                cols = slice(b * P, (b + 1) * P)
+                nc.tensor.matmul_mx(
+                    out=sides[b],
+                    lhsT=w2_codes[:, cols].bitcast(FP8X4),
+                    lhsT_scale=w2_scales[:, cols],
+                    rhs=h_tiles[s][1][:].bitcast(FP8X4),
+                    rhs_scale=h_tiles[s][2][:],
+                    start=True,
+                    stop=True,
+                )
+            accs[s] = acc
+
+        def leave(s, engine):
+            a, b = bounds[s]
+            res = keep.tile([P, 2, b - a], F32, name=f"res{s}")
+            if s == last:
+                nc.vector.tensor_copy(out=res[:, 0, :], in_=accs[s][0][:])
+                nc.scalar.copy(out=res[:, 1, :], in_=accs[s][1][:])
+            elif engine == "v":
+                nc.vector.tensor_copy(out=res[:], in_=accs[s][:])
+            else:
+                nc.scalar.copy(out=res[:], in_=accs[s][:])
+            nc.sync.dma_start(out=out_view[:, :, a:b], in_=res[:])
+
+        def cast_w2(b):
+            nc.vector.tensor_copy(
+                out=w2_grp[:, b * 4 * P : (b + 1) * 4 * P].rearrange("p (c i j) -> p c j i", i=4, j=4),
+                in_=w2_raw[:, :, b * P : (b + 1) * P].rearrange("p j (c i) -> p c j i", i=4),
+            )
+
+        gather(0, 0, V)
+        quantize(w1_codes, w1_scales, w1_grp, 0, H)
+        gather(1, 0, V)
+        gather(2, 0, V)
+        gather(3, 0, HALF)
+        quantize(x_codes, x_scales, x_flat, 0, 128)
+        quantize(x_codes, x_scales, x_flat, 128, 256)
+        first_product(0)
+        first_product(1)
+        gather(3, HALF, HALF)
+        cast_w2(0)
+        quantize(x_codes, x_scales, x_flat, 256, 384)
+        quantize(x_codes, x_scales, x_flat, 384, 512)
+        first_product(2)
+        first_product(3)
+        first_product(4)
+        cast_w2(1)
+        quantize_h(0)
+        quantize(w2_codes, w2_scales, w2_grp, 0, N)
+        quantize_h(1)
+        second_product(0)
+        second_product(1)
+        quantize_h(2)
+        second_product(2)
+        leave(0, "v")
+        quantize_h(3)
+        second_product(3)
+        leave(1, "v")
+        quantize_h(4)
+        second_product(4)
+        leave(2, "s")
+        leave(3, "v")
+        leave(4, "v")

@@ -70,7 +70,7 @@ def tile_picked_grid_mlp_silu_sub_l_kernel(tc, xT, w1, w2, offs, out):
 
         x_flat = x_grp[:].rearrange("p v j -> p (v j)")
         out_view = out.rearrange("(b p) v -> p b v", p=P)
-        bounds = [(0, 128), (128, 256), (256, 384), (384, 448), (448, 512)]
+        bounds = [(0, 128), (128, 256), (256, 384), (384, 512)]
         last = len(bounds) - 1
         h_tiles = {}
         accs = {}
@@ -150,30 +150,26 @@ def tile_picked_grid_mlp_silu_sub_l_kernel(tc, xT, w1, w2, offs, out):
         gather(2, 0, V)
         gather(3, 0, HALF)
         quantize(x_codes, x_scales, x_flat, 0, 128)
-        quantize(x_codes, x_scales, x_flat, 128, 256)
         first_product(0)
+        quantize(x_codes, x_scales, x_flat, 128, 256)
         first_product(1)
-        gather(3, HALF, HALF)
+        gather(3, HALF - 32, HALF + 32)
         cast_w2(0)
         quantize(x_codes, x_scales, x_flat, 256, 384)
-        quantize(x_codes, x_scales, x_flat, 384, 512)
         first_product(2)
+        quantize(x_codes, x_scales, x_flat, 384, 512)
         first_product(3)
-        first_product(4)
-        cast_w2(1)
         quantize_h(0)
-        quantize(w2_codes, w2_scales, w2_grp, 0, N)
+        cast_w2(1)
         quantize_h(1)
+        quantize(w2_codes, w2_scales, w2_grp, 0, N)
         second_product(0)
         second_product(1)
         quantize_h(2)
-        second_product(2)
         leave(0, "v")
+        second_product(2)
+        leave(1, "s")
         quantize_h(3)
         second_product(3)
-        leave(1, "v")
-        quantize_h(4)
-        second_product(4)
-        leave(2, "s")
+        leave(2, "v")
         leave(3, "v")
-        leave(4, "v")

from contextlib import ExitStack

import concourse.mybir as mybir

K, T, D, V, H, N = 512, 2048, 4, 512, 512, 256
FLOPS = 2 * K * H * V + 2 * H * N * V

F32 = mybir.dt.float32
BF16 = mybir.dt.bfloat16
U32 = mybir.dt.uint32
U16 = mybir.dt.uint16
U8 = mybir.dt.uint8
FP8X4 = mybir.dt.float8_e4m3fn_x4
SILU = mybir.ActivationFunctionType.Silu

P = 128
HALF = V // 2


def tile_picked_grid_mlp_silu_sub_l_kernel(tc, xT, w1, w2, offs, out):
    nc = tc.nc
    with ExitStack() as ctx:
        keep = ctx.enter_context(tc.tile_pool(name="keep", bufs=1))
        pre_pool = ctx.enter_context(tc.psum_pool(name="pre_pool", bufs=3))
        acc_pool = ctx.enter_context(tc.psum_pool(name="acc_pool", bufs=3))
        end_pool = ctx.enter_context(tc.psum_pool(name="end_pool", bufs=1))

        offsets = keep.tile([P, D * V // 16], U16, name="offsets")
        w1_raw = keep.tile([P, 4, H], F32, name="w1_raw")
        w2_raw = keep.tile([P, 4, N], F32, name="w2_raw")
        tables = [keep.tile([P, T], F32, name=f"table{l}") for l in range(D)]
        w1_grp = keep.tile([P, 4 * H], BF16, name="w1_grp", align_bytes=64)
        w2_grp = keep.tile([P, 4 * N], BF16, name="w2_grp", align_bytes=64)
        x_grp = keep.tile([P, V, 4], BF16, name="x_grp", align_bytes=64)
        w1_codes = keep.tile([P, H], U32, name="w1_codes", align_bytes=64)
        w1_scales = keep.tile([P, H], U8, name="w1_scales", align_bytes=64)
        w2_codes = keep.tile([P, N], U32, name="w2_codes", align_bytes=64)
        w2_scales = keep.tile([P, N], U8, name="w2_scales", align_bytes=64)
        x_codes = keep.tile([P, V], U32, name="x_codes", align_bytes=64)
        x_scales = keep.tile([P, V], U8, name="x_scales", align_bytes=64)
        dummy = keep.tile([P, 1], F32, name="dummy")
        dummy_out = keep.tile([P, 1], F32, name="dummy_out")

        nc.vector.memset(dummy[:], 0.0)
        nc.scalar.activation(dummy_out[:], dummy[:], SILU)

        x_levels = xT.rearrange("(f l) t -> l f t", l=D)
        nc.sync.dma_start(offsets[:], offs)
        nc.sync.dma_start(out=w1_raw[:], in_=w1.rearrange("(p j) i -> p j i", j=4))
        for l in range(D):
            nc.sync.dma_start(out=tables[l][:], in_=x_levels[l, :, :])
        nc.sync.dma_start(out=w2_raw[:], in_=w2.rearrange("(p j) m -> p j m", j=4))

        nc.scalar.copy(
            out=w1_grp[:].rearrange("p (t m j) -> p m j t", t=4, j=4),
            in_=w1_raw[:].rearrange("p j (m t) -> p m j t", t=4),
        )

        def gather(l, v0, n):
            c0 = (l * V + v0) // 16
            nc.vector.tensor_copy(
                x_grp[:, v0 : v0 + n, l],
                tables[l][:].indirect(offsets[:, c0 : c0 + n // 16]),
            )

        def quantize(codes, scales, grouped, a, b):
            nc.vector.quantize_mx(
                out=codes[:, a:b].bitcast(FP8X4), scales=scales[:, a:b], in_=grouped[:, 4 * a : 4 * b]
            )

        x_flat = x_grp[:].rearrange("p v j -> p (v j)")
        out_view = out.rearrange("(b p) v -> p b v", p=P)
        bounds = [(0, 128), (128, 256), (256, 384), (384, 512)]
        last = len(bounds) - 1
        h_tiles = {}
        accs = {}

        def first_product(s):
            a, b = bounds[s]
            n = b - a
            pre = pre_pool.tile([P, 4, n], F32, name="pre")
            for t in range(4):
                cols = slice(t * P, (t + 1) * P)
                nc.tensor.matmul_mx(
                    out=pre[:, t, :],
                    lhsT=w1_codes[:, cols].bitcast(FP8X4),
                    lhsT_scale=w1_scales[:, cols],
                    rhs=x_codes[:, a:b].bitcast(FP8X4),
                    rhs_scale=x_scales[:, a:b],
                    start=True,
                    stop=True,
                )
            h_grp = keep.tile([P, 4 * n], BF16, name=f"h_grp{s}", align_bytes=64)
            nc.scalar.activation(
                h_grp[:].rearrange("p (v t) -> p v t", t=4), pre[:].rearrange("p t v -> p v t"), SILU
            )
            h_tiles[s] = [h_grp]

        def quantize_h(s):
            n = bounds[s][1] - bounds[s][0]
            h_codes = keep.tile([P, n], U32, name=f"h_codes{s}", align_bytes=64)
            h_scales = keep.tile([P, n], U8, name=f"h_scales{s}", align_bytes=64)
            quantize(h_codes, h_scales, h_tiles[s][0], 0, n)
            h_tiles[s] += [h_codes, h_scales]

        def second_product(s):
            n = bounds[s][1] - bounds[s][0]
            if s < last:
                acc = acc_pool.tile([P, 2, n], F32, name="acc")
                sides = [acc[:, 0, :], acc[:, 1, :]]
            else:
                end0 = end_pool.tile([P, n], F32, name="end0")
                end1 = end_pool.tile([P, n], F32, name="end1")
                acc = (end0, end1)
                sides = [end0[:], end1[:]]
            for b in range(2):
                cols = slice(b * P, (b + 1) * P)
                nc.tensor.matmul_mx(
                    out=sides[b],
                    lhsT=w2_codes[:, cols].bitcast(FP8X4),
                    lhsT_scale=w2_scales[:, cols],
                    rhs=h_tiles[s][1][:].bitcast(FP8X4),
                    rhs_scale=h_tiles[s][2][:],
                    start=True,
                    stop=True,
                )
            accs[s] = acc

        def leave(s, engine):
            a, b = bounds[s]
            res = keep.tile([P, 2, b - a], F32, name=f"res{s}")
            if s == last:
                nc.vector.tensor_copy(out=res[:, 0, :], in_=accs[s][0][:])
                nc.scalar.copy(out=res[:, 1, :], in_=accs[s][1][:])
            elif engine == "v":
                nc.vector.tensor_copy(out=res[:], in_=accs[s][:])
            else:
                nc.scalar.copy(out=res[:], in_=accs[s][:])
            nc.sync.dma_start(out=out_view[:, :, a:b], in_=res[:])

        def cast_w2(b):
            nc.vector.tensor_copy(
                out=w2_grp[:, b * 4 * P : (b + 1) * 4 * P].rearrange("p (c i j) -> p c j i", i=4, j=4),
                in_=w2_raw[:, :, b * P : (b + 1) * P].rearrange("p j (c i) -> p c j i", i=4),
            )

        gather(0, 0, V)
        quantize(w1_codes, w1_scales, w1_grp, 0, H)
        gather(1, 0, V)
        gather(2, 0, V)
        gather(3, 0, HALF)
        quantize(x_codes, x_scales, x_flat, 0, 128)
        first_product(0)
        quantize(x_codes, x_scales, x_flat, 128, 256)
        first_product(1)
        gather(3, HALF - 32, HALF + 32)
        cast_w2(0)
        quantize(x_codes, x_scales, x_flat, 256, 384)
        first_product(2)
        quantize(x_codes, x_scales, x_flat, 384, 512)
        first_product(3)
        quantize_h(0)
        cast_w2(1)
        quantize_h(1)
        quantize(w2_codes, w2_scales, w2_grp, 0, N)
        second_product(0)
        second_product(1)
        quantize_h(2)
        leave(0, "v")
        second_product(2)
        leave(1, "s")
        quantize_h(3)
        second_product(3)
        leave(2, "v")
        leave(3, "v")
